import numpy as np
import ml_dtypes


def mxq(x, axis, fmt="e4m3"):
    dtype, down = {"e4m3": (ml_dtypes.float8_e4m3fn, 7), "e5m2": (ml_dtypes.float8_e5m2, 14)}[fmt]
    v = np.moveaxis(np.asarray(x, np.float32).astype(ml_dtypes.bfloat16).astype(np.float64), axis, -1)
    blocks = v.reshape(v.shape[:-1] + (-1, 32))
    amax = np.abs(blocks).max(-1, keepdims=True)
    byte = np.maximum(np.where(amax > 0, np.frexp(amax)[1] - 1 + 127, 0) - down, 1)
    scale = np.exp2(byte - 127.0)
    codes = (blocks / scale).astype(np.float32).astype(dtype).astype(np.float64)
    return np.moveaxis((codes * scale).reshape(v.shape), -1, axis)


WIDE = False


def mx_kscale(k):
    if not WIDE:
        return np.ones(k)
    levels = np.array([10, -10, 5, -5, 0])
    if k % 512:
        return np.exp2(np.random.permutation(np.resize(levels, k // 32))).repeat(32)
    a = np.empty((k // 512, 16))
    for p in range(k // 512):
        a[p, :8] = np.random.permutation(np.resize(levels, 8))
        for g in range(8):
            far = levels[np.abs(levels - a[p, g]) >= 10]
            a[p, g + 8] = far[np.random.randint(len(far))]
    return np.exp2(a.ravel()).repeat(32)


def f64(x):
    return np.asarray(x).astype(np.float64)


def striped(idx):
    return np.tile(np.asarray(idx).reshape(-1, 16).T, (8, 1)).astype(np.uint16)


def unstriped(offs):
    return offs[:16].T.reshape(-1).astype(np.int64)


E2M1 = np.array([0.0, 0.5, 1.0, 1.5, 2.0, 3.0, 4.0, 6.0, -0.0, -0.5, -1.0, -1.5, -2.0, -3.0, -4.0, -6.0])


def pack_weight(w, fmt):
    k, n = w.shape
    w = f64(np.asarray(w, np.float32).astype(ml_dtypes.bfloat16)).reshape(k // 32, 32, n)
    amax = np.abs(w).max(1)
    if fmt == "e4m3":
        byte = np.frexp(amax)[1] - 1 + 127 - 7
    else:
        mant, ex = np.frexp(amax / 6.0)
        byte = np.where(mant > 0.5, ex, ex - 1) + 127
    byte = np.clip(np.where(amax > 0, byte, 1), 1, 254)
    scaled = (w * np.exp2(127.0 - byte)[:, None, :]).reshape(k, n).astype(np.float32)
    by_word = np.ascontiguousarray(scaled.reshape(k // 512, 128, 4, n).transpose(0, 1, 3, 2))
    if fmt == "e4m3":
        words = by_word.astype(ml_dtypes.float8_e4m3fn).view(np.uint8)
    else:
        c = by_word.astype(ml_dtypes.float4_e2m1fn).view(np.uint8) & 0xF
        words = (c[..., 0::2] | (c[..., 1::2] << 4)).reshape(k // 512, 128, 2 * n)
    return np.ascontiguousarray(words), np.ascontiguousarray(byte.astype(np.uint8).reshape(k // 512, 16, n))


def unpack_weight(words, scales, fmt):
    g, _, n = scales.shape
    words = np.ascontiguousarray(words).reshape(g, 128, n, -1)
    if fmt == "e4m3":
        vals = words.view(ml_dtypes.float8_e4m3fn).astype(np.float64)
    else:
        nib = np.empty((g, 128, n, 4), np.uint8)
        nib[..., 0::2] = words & 0xF
        nib[..., 1::2] = words >> 4
        vals = E2M1[nib]
    vals = vals * np.repeat(np.exp2(scales.astype(np.float64) - 127.0), 8, axis=1)[..., None]
    return vals.transpose(0, 1, 3, 2).reshape(g * 512, n)


K, T, J, I, N, M = 1024, 1024, 512, 512, 512, 512


def setup_inputs():
    n = np.random.standard_normal
    idx = np.random.permutation(T)[:J]
    idx2 = np.random.permutation(T)[:I]
    fk = mx_kscale(K)
    fn = mx_kscale(N)
    xqp = pack_weight(n((K, T)) / fk[:, None], "e4m3")
    wap = pack_weight(n((K, N)) * 1 / np.sqrt(K) * fk[:, None] * fn, "e2m1")
    wmp = pack_weight(n((N, M)) * 1 / np.sqrt(N) / fn[:, None], "e4m3")
    return {
        "xq_words": xqp[0],
        "xq_scales": xqp[1],
        "wa_words": wap[0],
        "wa_scales": wap[1],
        "res": (n((N, T)) * fn[:, None]).astype(np.float32),
        "wm_words": wmp[0],
        "wm_scales": wmp[1],
        "b": (np.random.uniform(-0.5, 0.5, (M, 1))).astype(np.float32),
        "offs": striped(idx),
        "offs2": striped(idx2),
    }


def reference(xq_words, xq_scales, wa_words, wa_scales, res, wm_words, wm_scales, b, offs, offs2):
    idx = unstriped(offs)
    idx2 = unstriped(offs2)
    xqu = unpack_weight(xq_words, xq_scales, "e4m3")
    wau = unpack_weight(wa_words, wa_scales, "e2m1")
    wmu = unpack_weight(wm_words, wm_scales, "e4m3")
    xqidxg = xqu[:, idx]
    p = wau.T @ xqidxg
    pg = np.zeros((N, T))
    pg[:, idx] = p
    up = f64(res) + pg
    us = up[:, idx2]
    usq = mxq(us, 0, "e4m3")
    z = wmu.T @ usq
    y = np.maximum(z + f64(b), 0.0)
    return y

@@ -1,0 +1,221 @@
+from contextlib import ExitStack
+
+import concourse.mybir as mybir
+from concourse.masks import make_identity
+
+K, T, J, I, N, M = 1024, 1024, 512, 512, 512, 512
+FLOPS = 2 * K * N * J + 2 * N * M * I
+
+F32 = mybir.dt.float32
+BF16 = mybir.dt.bfloat16
+I32 = mybir.dt.int32
+U32 = mybir.dt.uint32
+U16 = mybir.dt.uint16
+U8 = mybir.dt.uint8
+FP8X4 = mybir.dt.float8_e4m3fn_x4
+FP4X4 = mybir.dt.float4_e2m1fn_x4
+ADD = mybir.AluOpType.add
+MAX = mybir.AluOpType.max
+COPY = mybir.ActivationFunctionType.Copy
+RELU = mybir.ActivationFunctionType.Relu
+
+P = 128
+PACK = 4
+PASSES = K // (P * PACK)
+BANK = 512
+HALF = 256
+PAGES = 3
+ADD_ON = "pe"
+
+
+def load_plane(nc, plane, scales):
+    for q in range(4):
+        nc.sync.dma_start(
+            out=plane[32 * q : 32 * q + 4].bitcast(I32),
+            in_=scales[:, 4 * q : 4 * q + 4, :].rearrange("z r c -> r z c").bitcast(I32),
+        )
+
+
+def tile_list_second_reads_updated_page_kernel(
+    tc, xq_words, xq_scales, wa_words, wa_scales, res, wm_words, wm_scales, b, offs, offs2, out
+):
+    nc = tc.nc
+    with ExitStack() as ctx:
+        keep = ctx.enter_context(tc.tile_pool(name="keep", bufs=1))
+        psum = ctx.enter_context(tc.psum_pool(name="psum", bufs=1))
+
+        def bank(index):
+            return psum.tile([P, BANK], F32, name="bank%d" % index)
+
+        list1 = keep.tile([P, J // 16], U16, name="list1")
+        list2 = keep.tile([P, I // 16], U16, name="list2")
+        xq_plane = keep.tile([P, PASSES, T], U8, name="xq_plane", align_bytes=64)
+        wa_plane_raw = keep.tile([P, PASSES, N], U8, name="wa_plane_raw", align_bytes=64)
+        wm_plane = keep.tile([P, 1, M], U8, name="wm_plane", align_bytes=64)
+        wa_raw = keep.tile([P, PASSES, 2 * N], U8, name="wa_raw", align_bytes=64)
+        xq_tab = [keep.tile([P, T], I32, name="xq_tab%d" % z, align_bytes=64) for z in range(PASSES)]
+        res_t = [keep.tile([P, T], F32, name="res%d" % t, align_bytes=64) for t in range(PACK)]
+        wm_codes = keep.tile([P, M], I32, name="wm_codes", align_bytes=64)
+        bias = keep.tile([P, M // P], F32, name="bias")
+        pages = [keep.tile([P, T], F32, name="page%d" % g, align_bytes=64) for g in range(PAGES)]
+
+        for plane in (xq_plane, wa_plane_raw, wm_plane):
+            nc.vector.memset(plane[:].bitcast(I32), 0)
+        for page in pages:
+            nc.vector.memset(page[:], 0.0)
+        if ADD_ON == "pe":
+            ident = keep.tile([P, P], F32, name="ident", align_bytes=64)
+            make_identity(nc, ident[:])
+
+        nc.sync.dma_start(out=list1[:], in_=offs)
+        nc.sync.dma_start(out=wa_raw[:].bitcast(I32), in_=wa_words.rearrange("z p c -> p z c").bitcast(I32))
+        nc.sync.dma_start(out=xq_tab[0][:], in_=xq_words[0].rearrange("p c r -> p (c r)").bitcast(I32))
+        load_plane(nc, xq_plane, xq_scales)
+        nc.sync.dma_start(out=xq_tab[1][:], in_=xq_words[1].rearrange("p c r -> p (c r)").bitcast(I32))
+        load_plane(nc, wa_plane_raw, wa_scales)
+        res_rows = res.rearrange("(p t) c -> t p c", t=PACK)
+        for t in range(PACK):
+            nc.sync.dma_start(out=res_t[t][:], in_=res_rows[t])
+        nc.sync.dma_start(out=list2[:], in_=offs2)
+        nc.sync.dma_start(out=wm_codes[:], in_=wm_words[0].rearrange("p c r -> p (c r)").bitcast(I32))
+        load_plane(nc, wm_plane, wm_scales)
+        with nc.allow_non_contiguous_dma(reason="one bias value a partition"):
+            nc.sync.dma_start(out=bias[:], in_=b.rearrange("(c p) o -> p (c o)", p=P))
+
+        wa_codes = keep.tile([P, PASSES, 2 * N], U8, name="wa_codes", align_bytes=64)
+        wa_plane = keep.tile([P, PASSES, N], U8, name="wa_plane", align_bytes=64)
+        x_codes = [keep.tile([P, J], U32, name="x_codes%d" % z, align_bytes=64) for z in range(PASSES)]
+        x_plane = [keep.tile([P, J], U8, name="x_plane%d" % z, align_bytes=64) for z in range(PASSES)]
+
+        def gather_codes(z, h):
+            nc.vector.tensor_copy(
+                x_codes[z][:, h * HALF : (h + 1) * HALF],
+                xq_tab[z][:].bitcast(U32).indirect(list1[:, h * 16 : (h + 1) * 16]),
+            )
+
+        def gather_plane(z, h):
+            nc.vector.tensor_copy(
+                x_plane[z][:, h * HALF : (h + 1) * HALF],
+                xq_plane[:, z, :].indirect(list1[:, h * 16 : (h + 1) * 16]),
+            )
+
+        nc.vector.tensor_copy(
+            wa_codes[:].bitcast(U16).rearrange("p z (t m) -> p z t m", t=PACK),
+            wa_raw[:].bitcast(U16).rearrange("p z (m t) -> p z t m", t=PACK),
+        )
+        gather_codes(0, 0)
+        gather_codes(0, 1)
+        gather_plane(0, 0)
+        gather_plane(1, 0)
+        nc.vector.tensor_copy(
+            wa_plane[:].rearrange("p z (t m) -> p z t m", t=PACK),
+            wa_plane_raw[:].rearrange("p z (m t) -> p z t m", t=PACK),
+        )
+        gather_codes(1, 0)
+        gather_plane(0, 1)
+        gather_plane(1, 1)
+        gather_codes(1, 1)
+
+        def first_product(acc, t, lo, width):
+            for z in range(PASSES):
+                nc.tensor.matmul_mx(
+                    out=acc,
+                    lhsT=wa_codes[:, z, 2 * P * t : 2 * P * (t + 1)].bitcast(FP4X4),
+                    lhsT_scale=wa_plane[:, z, P * t : P * (t + 1)],
+                    rhs=x_codes[z][:, lo : lo + width].bitcast(FP8X4),
+                    rhs_scale=x_plane[z][:, lo : lo + width],
+                    start=(z == 0),
+                    stop=(z == PASSES - 1),
+                )
+
+        p_first = []
+        for h in range(2):
+            acc = bank(h)
+            for c in range(HALF // P):
+                first_product(acc[:, c * P : (c + 1) * P], 0, h * HALF + c * P, P)
+            p_half = keep.tile([P, HALF], F32, name="p0_%d" % h, align_bytes=64)
+            nc.scalar.activation(p_half[:], acc[:, 0:HALF], COPY)
+            p_first.append(p_half)
+        p_rest = []
+        for t in range(1, PACK):
+            acc = bank((t + 1) % 4)
+            first_product(acc[:], t, 0, J)
+            p_t = keep.tile([P, J], F32, name="p%d" % t, align_bytes=64)
+            nc.scalar.copy(p_t[:], acc[:])
+            p_rest.append(p_t)
+
+        up = [keep.tile([P, T], F32, name="up%d" % t, align_bytes=64) for t in range(PACK)]
+        turned = [keep.tile([P, BANK], F32, name="turned%d" % a, align_bytes=64) for a in range(2)]
+        for t in range(PACK):
+            page = pages[t % PAGES]
+            if t == 0:
+                for h in range(2):
+                    nc.vector.tensor_copy(page[:].indirect(list1[:, h * 16 : (h + 1) * 16]), p_first[h][:])
+            else:
+                nc.vector.tensor_copy(page[:].indirect(list1[:]), p_rest[t - 1][:])
+            if ADD_ON == "pe":
+                for a in range(2):
+                    acc = bank(4 + a)
+                    for n, source in enumerate((res_t[t], page)):
+                        for c in range(4):
+                            nc.tensor.matmul(
+                                acc[:, c * P : (c + 1) * P],
+                                source[:, a * BANK + c * P : a * BANK + (c + 1) * P],
+                                ident[:],
+                                start=(n == 0 and c == 0),
+                                stop=(n == 1 and c == 3),
+                                is_transpose=True,
+                            )
+                    nc.scalar.copy(turned[a][:], acc[:])
+                for a in range(2):
+                    back = bank(6 + a)
+                    for c in range(4):
+                        nc.tensor.transpose(back[:, c * P : (c + 1) * P], turned[a][:, c * P : (c + 1) * P], ident[:])
+                    nc.scalar.copy(up[t][:, a * BANK : (a + 1) * BANK], back[:])
+            else:
+                nc.gpsimd.tensor_tensor(up[t][:], res_t[t][:], page[:], ADD)
+
+        picked = keep.tile([P, 2, PACK, HALF], BF16, name="picked", align_bytes=64)
+        for t in range(PACK - 1):
+            nc.vector.tensor_copy(picked[:, :, t, :], up[t][:].indirect(list2[:]))
+        for h in range(2):
+            nc.vector.tensor_copy(picked[:, h, PACK - 1, :], up[PACK - 1][:].indirect(list2[:, h * 16 : (h + 1) * 16]))
+
+        woven = [keep.tile([P, HALF, PACK], BF16, name="woven%d" % h, align_bytes=64) for h in range(2)]
+        for h in range(2):
+            dst = woven[h][:].rearrange("p (c i) t -> p c t i", i=4)
+            src = picked[:, h].rearrange("p t (c i) -> p c t i", i=4)
+            if h == 0:
+                nc.scalar.copy(dst, src)
+            else:
+                nc.vector.tensor_copy(dst, src)
+        out_rows = out.rearrange("(c p) i -> p c i", p=P)
+        for h in range(2):
+            u_codes = keep.tile([P, HALF], U32, name="u_codes%d" % h, align_bytes=64)
+            u_plane = keep.tile([P, HALF], U8, name="u_plane%d" % h, align_bytes=64)
+            nc.vector.quantize_mx(
+                out=u_codes[:].bitcast(FP8X4), scales=u_plane[:], in_=woven[h][:].rearrange("p c t -> p (c t)")
+            )
+            for g in range(2):
+                acc = bank(2 * h + g)
+                y = keep.tile([P, 2, HALF], F32, name="y%d_%d" % (h, g), align_bytes=64)
+                for e in range(2):
+                    c = 2 * g + e
+                    nc.tensor.matmul_mx(
+                        out=acc[:, e * HALF : (e + 1) * HALF],
+                        lhsT=wm_codes[:, c * P : (c + 1) * P].bitcast(FP8X4),
+                        lhsT_scale=wm_plane[:, 0, c * P : (c + 1) * P],
+                        rhs=u_codes[:].bitcast(FP8X4),
+                        rhs_scale=u_plane[:],
+                        start=True,
+                        stop=True,
+                    )
+                for e in range(2):
+                    c = 2 * g + e
+                    if g == 0 or h == 0:
+                        nc.scalar.activation(y[:, e, :], acc[:, e * HALF : (e + 1) * HALF], RELU, bias=bias[:, c : c + 1])
+                    else:
+                        nc.vector.tensor_scalar(
+                            y[:, e, :], acc[:, e * HALF : (e + 1) * HALF], bias[:, c : c + 1], 0.0, ADD, MAX
+                        )
+                nc.sync.dma_start(out=out_rows[:, 2 * g : 2 * g + 2, h * HALF : (h + 1) * HALF], in_=y[:])

@@ -25,7 +25,7 @@ PASSES = K // (P * PACK)
 BANK = 512
 HALF = 256
 PAGES = 3
-ADD_ON = "pe"
+ADD_ON = "pool"
 
 
 def load_plane(nc, plane, scales):
@@ -53,7 +53,7 @@ def tile_list_second_reads_updated_page_kernel(
         wa_plane_raw = keep.tile([P, PASSES, N], U8, name="wa_plane_raw", align_bytes=64)
         wm_plane = keep.tile([P, 1, M], U8, name="wm_plane", align_bytes=64)
         wa_raw = keep.tile([P, PASSES, 2 * N], U8, name="wa_raw", align_bytes=64)
-        xq_tab = [keep.tile([P, T], I32, name="xq_tab%d" % z, align_bytes=64) for z in range(PASSES)]
+        xq_tab = keep.tile([P, PASSES, T], I32, name="xq_tab", align_bytes=64)
         res_t = [keep.tile([P, T], F32, name="res%d" % t, align_bytes=64) for t in range(PACK)]
         wm_codes = keep.tile([P, M], I32, name="wm_codes", align_bytes=64)
         bias = keep.tile([P, M // P], F32, name="bias")
@@ -69,10 +69,9 @@ def tile_list_second_reads_updated_page_kernel(
 
         nc.sync.dma_start(out=list1[:], in_=offs)
         nc.sync.dma_start(out=wa_raw[:].bitcast(I32), in_=wa_words.rearrange("z p c -> p z c").bitcast(I32))
-        nc.sync.dma_start(out=xq_tab[0][:], in_=xq_words[0].rearrange("p c r -> p (c r)").bitcast(I32))
         load_plane(nc, xq_plane, xq_scales)
-        nc.sync.dma_start(out=xq_tab[1][:], in_=xq_words[1].rearrange("p c r -> p (c r)").bitcast(I32))
         load_plane(nc, wa_plane_raw, wa_scales)
+        nc.sync.dma_start(out=xq_tab[:], in_=xq_words.rearrange("z p c r -> p z (c r)").bitcast(I32))
         res_rows = res.rearrange("(p t) c -> t p c", t=PACK)
         for t in range(PACK):
             nc.sync.dma_start(out=res_t[t][:], in_=res_rows[t])
@@ -90,31 +89,25 @@ def tile_list_second_reads_updated_page_kernel(
         def gather_codes(z, h):
             nc.vector.tensor_copy(
                 x_codes[z][:, h * HALF : (h + 1) * HALF],
-                xq_tab[z][:].bitcast(U32).indirect(list1[:, h * 16 : (h + 1) * 16]),
+                xq_tab[:, z, :].bitcast(U32).indirect(list1[:, h * 16 : (h + 1) * 16]),
             )
 
-        def gather_plane(z, h):
-            nc.vector.tensor_copy(
-                x_plane[z][:, h * HALF : (h + 1) * HALF],
-                xq_plane[:, z, :].indirect(list1[:, h * 16 : (h + 1) * 16]),
-            )
+        def gather_plane(z):
+            nc.vector.tensor_copy(x_plane[z][:], xq_plane[:, z, :].indirect(list1[:]))
 
         nc.vector.tensor_copy(
             wa_codes[:].bitcast(U16).rearrange("p z (t m) -> p z t m", t=PACK),
             wa_raw[:].bitcast(U16).rearrange("p z (m t) -> p z t m", t=PACK),
         )
-        gather_codes(0, 0)
-        gather_codes(0, 1)
-        gather_plane(0, 0)
-        gather_plane(1, 0)
+        gather_plane(0)
+        gather_plane(1)
         nc.vector.tensor_copy(
             wa_plane[:].rearrange("p z (t m) -> p z t m", t=PACK),
             wa_plane_raw[:].rearrange("p z (m t) -> p z t m", t=PACK),
         )
-        gather_codes(1, 0)
-        gather_plane(0, 1)
-        gather_plane(1, 1)
-        gather_codes(1, 1)
+        for h in range(2):
+            for z in range(PASSES):
+                gather_codes(z, h)
 
         def first_product(acc, t, lo, width):
             for z in range(PASSES):
@@ -176,10 +169,11 @@ def tile_list_second_reads_updated_page_kernel(
                 nc.gpsimd.tensor_tensor(up[t][:], res_t[t][:], page[:], ADD)
 
         picked = keep.tile([P, 2, PACK, HALF], BF16, name="picked", align_bytes=64)
-        for t in range(PACK - 1):
+        for t in range(2):
             nc.vector.tensor_copy(picked[:, :, t, :], up[t][:].indirect(list2[:]))
         for h in range(2):
-            nc.vector.tensor_copy(picked[:, h, PACK - 1, :], up[PACK - 1][:].indirect(list2[:, h * 16 : (h + 1) * 16]))
+            for t in range(2, PACK):
+                nc.vector.tensor_copy(picked[:, h, t, :], up[t][:].indirect(list2[:, h * 16 : (h + 1) * 16]))
 
         woven = [keep.tile([P, HALF, PACK], BF16, name="woven%d" % h, align_bytes=64) for h in range(2)]
         for h in range(2):

@@ -1,7 +1,6 @@
 from contextlib import ExitStack
 
 import concourse.mybir as mybir
-from concourse.masks import make_identity
 
 K, T, J, I, N, M = 1024, 1024, 512, 512, 512, 512
 FLOPS = 2 * K * N * J + 2 * N * M * I
@@ -23,9 +22,11 @@ P = 128
 PACK = 4
 PASSES = K // (P * PACK)
 BANK = 512
-HALF = 256
+HALF = J // 2
 PAGES = 3
-ADD_ON = "pool"
+PIECE = 128
+PIECES = I // PIECE
+SLOTS = 6
 
 
 def load_plane(nc, plane, scales):
@@ -36,180 +37,195 @@ def load_plane(nc, plane, scales):
         )
 
 
+def entries(offsets, first, count):
+    return offsets[:, first // 16 : (first + count) // 16]
+
+
 def tile_list_second_reads_updated_page_kernel(
     tc, xq_words, xq_scales, wa_words, wa_scales, res, wm_words, wm_scales, b, offs, offs2, out
 ):
     nc = tc.nc
     with ExitStack() as ctx:
+        lists = ctx.enter_context(tc.tile_pool(name="lists", bufs=1))
         keep = ctx.enter_context(tc.tile_pool(name="keep", bufs=1))
         psum = ctx.enter_context(tc.psum_pool(name="psum", bufs=1))
 
         def bank(index):
             return psum.tile([P, BANK], F32, name="bank%d" % index)
 
-        list1 = keep.tile([P, J // 16], U16, name="list1")
-        list2 = keep.tile([P, I // 16], U16, name="list2")
-        xq_plane = keep.tile([P, PASSES, T], U8, name="xq_plane", align_bytes=64)
-        wa_plane_raw = keep.tile([P, PASSES, N], U8, name="wa_plane_raw", align_bytes=64)
-        wm_plane = keep.tile([P, 1, M], U8, name="wm_plane", align_bytes=64)
-        wa_raw = keep.tile([P, PASSES, 2 * N], U8, name="wa_raw", align_bytes=64)
-        xq_tab = keep.tile([P, PASSES, T], I32, name="xq_tab", align_bytes=64)
-        res_t = [keep.tile([P, T], F32, name="res%d" % t, align_bytes=64) for t in range(PACK)]
-        wm_codes = keep.tile([P, M], I32, name="wm_codes", align_bytes=64)
-        bias = keep.tile([P, M // P], F32, name="bias")
-        pages = [keep.tile([P, T], F32, name="page%d" % g, align_bytes=64) for g in range(PAGES)]
+        def room(name, shape, dtype, tag=None):
+            return keep.tile(shape, dtype, name=name, tag=tag or name, align_bytes=64)
 
-        for plane in (xq_plane, wa_plane_raw, wm_plane):
-            nc.vector.memset(plane[:].bitcast(I32), 0)
-        for page in pages:
-            nc.vector.memset(page[:], 0.0)
-        if ADD_ON == "pe":
-            ident = keep.tile([P, P], F32, name="ident", align_bytes=64)
-            make_identity(nc, ident[:])
+        list1 = lists.tile([P, J // 16], U16, name="list1")
+        list2 = lists.tile([P, I // 16], U16, name="list2")
+        xq_plane = room("xq_plane", [P, PASSES, T], U8)
+        wa_plane_raw = room("wa_plane_raw", [P, PASSES, N], U8)
+        wa_raw = [room("wa_raw%d" % z, [P, 2 * N], U8) for z in range(PASSES)]
+        xq_tab = room("xq_tab", [P, PASSES, T], I32)
+        pages = [room("page0", [P, T], F32)]
+
+        nc.vector.memset(xq_plane[:, 0, :].bitcast(I32), 0)
+        nc.gpsimd.memset(xq_plane[:, 1, :].bitcast(I32), 0)
+        nc.vector.memset(wa_plane_raw[:].bitcast(I32), 0)
+        nc.vector.memset(pages[0][:], 0.0)
 
         nc.sync.dma_start(out=list1[:], in_=offs)
-        nc.sync.dma_start(out=wa_raw[:].bitcast(I32), in_=wa_words.rearrange("z p c -> p z c").bitcast(I32))
+        for z in range(PASSES):
+            nc.sync.dma_start(out=wa_raw[z][:].bitcast(I32), in_=wa_words[z].bitcast(I32))
+        nc.sync.dma_start(out=list2[:], in_=offs2)
         load_plane(nc, xq_plane, xq_scales)
         load_plane(nc, wa_plane_raw, wa_scales)
         nc.sync.dma_start(out=xq_tab[:], in_=xq_words.rearrange("z p c r -> p z (c r)").bitcast(I32))
-        res_rows = res.rearrange("(p t) c -> t p c", t=PACK)
-        for t in range(PACK):
-            nc.sync.dma_start(out=res_t[t][:], in_=res_rows[t])
-        nc.sync.dma_start(out=list2[:], in_=offs2)
-        nc.sync.dma_start(out=wm_codes[:], in_=wm_words[0].rearrange("p c r -> p (c r)").bitcast(I32))
-        load_plane(nc, wm_plane, wm_scales)
-        with nc.allow_non_contiguous_dma(reason="one bias value a partition"):
-            nc.sync.dma_start(out=bias[:], in_=b.rearrange("(c p) o -> p (c o)", p=P))
 
-        wa_codes = keep.tile([P, PASSES, 2 * N], U8, name="wa_codes", align_bytes=64)
-        wa_plane = keep.tile([P, PASSES, N], U8, name="wa_plane", align_bytes=64)
-        x_codes = [keep.tile([P, J], U32, name="x_codes%d" % z, align_bytes=64) for z in range(PASSES)]
-        x_plane = [keep.tile([P, J], U8, name="x_plane%d" % z, align_bytes=64) for z in range(PASSES)]
+        wa_codes = room("wa_codes", [P, PASSES, 2 * N], U8)
+        wa_plane = room("wa_plane", [P, PASSES, N], U8)
+        x_codes = [room("x_codes%d" % z, [P, J], U32) for z in range(PASSES)]
+        x_plane = [room("x_plane%d" % z, [P, J], U8) for z in range(PASSES)]
 
-        def gather_codes(z, h):
+        for z in range(PASSES):
             nc.vector.tensor_copy(
-                x_codes[z][:, h * HALF : (h + 1) * HALF],
-                xq_tab[:, z, :].bitcast(U32).indirect(list1[:, h * 16 : (h + 1) * 16]),
+                wa_codes[:, z, :].bitcast(U16).rearrange("p (t m) -> p t m", t=PACK),
+                wa_raw[z][:].bitcast(U16).rearrange("p (m t) -> p t m", t=PACK),
             )
-
-        def gather_plane(z):
+        for z in range(PASSES):
             nc.vector.tensor_copy(x_plane[z][:], xq_plane[:, z, :].indirect(list1[:]))
-
-        nc.vector.tensor_copy(
-            wa_codes[:].bitcast(U16).rearrange("p z (t m) -> p z t m", t=PACK),
-            wa_raw[:].bitcast(U16).rearrange("p z (m t) -> p z t m", t=PACK),
-        )
-        gather_plane(0)
-        gather_plane(1)
         nc.vector.tensor_copy(
             wa_plane[:].rearrange("p z (t m) -> p z t m", t=PACK),
             wa_plane_raw[:].rearrange("p z (m t) -> p z t m", t=PACK),
         )
         for h in range(2):
             for z in range(PASSES):
-                gather_codes(z, h)
+                nc.vector.tensor_copy(
+                    x_codes[z][:, h * HALF : (h + 1) * HALF],
+                    xq_tab[:, z, :].bitcast(U32).indirect(entries(list1, h * HALF, HALF)),
+                )
 
-        def first_product(acc, t, lo, width):
-            for z in range(PASSES):
+        for tenant in ("wa_plane_raw", "xq_tab"):
+            page = room("page%d" % len(pages), [P, T], F32, tag=tenant)
+            nc.gpsimd.memset(page[:], 0.0)
+            pages.append(page)
+
+        def first_product(acc, t, first, count, width):
+            steps = [(z, lo) for z in range(PASSES) for lo in range(0, count, width)]
+            for z, lo in steps:
                 nc.tensor.matmul_mx(
-                    out=acc,
+                    out=acc[:, lo : lo + width],
                     lhsT=wa_codes[:, z, 2 * P * t : 2 * P * (t + 1)].bitcast(FP4X4),
                     lhsT_scale=wa_plane[:, z, P * t : P * (t + 1)],
-                    rhs=x_codes[z][:, lo : lo + width].bitcast(FP8X4),
-                    rhs_scale=x_plane[z][:, lo : lo + width],
-                    start=(z == 0),
-                    stop=(z == PASSES - 1),
+                    rhs=x_codes[z][:, first + lo : first + lo + width].bitcast(FP8X4),
+                    rhs_scale=x_plane[z][:, first + lo : first + lo + width],
+                    start=((z, lo) == steps[0]),
+                    stop=((z, lo) == steps[-1]),
                 )
 
         p_first = []
         for h in range(2):
             acc = bank(h)
-            for c in range(HALF // P):
-                first_product(acc[:, c * P : (c + 1) * P], 0, h * HALF + c * P, P)
-            p_half = keep.tile([P, HALF], F32, name="p0_%d" % h, align_bytes=64)
+            first_product(acc, 0, h * HALF, HALF, P)
+            p_half = room("p0_%d" % h, [P, HALF], F32)
             nc.scalar.activation(p_half[:], acc[:, 0:HALF], COPY)
             p_first.append(p_half)
         p_rest = []
         for t in range(1, PACK):
-            acc = bank((t + 1) % 4)
-            first_product(acc[:], t, 0, J)
-            p_t = keep.tile([P, J], F32, name="p%d" % t, align_bytes=64)
+            acc = bank(t + 1)
+            first_product(acc, t, 0, J, J)
+            p_t = room("p%d" % t, [P, J], F32)
             nc.scalar.copy(p_t[:], acc[:])
             p_rest.append(p_t)
 
-        up = [keep.tile([P, T], F32, name="up%d" % t, align_bytes=64) for t in range(PACK)]
-        turned = [keep.tile([P, BANK], F32, name="turned%d" % a, align_bytes=64) for a in range(2)]
+        res_rows = res.rearrange("(p t) c -> t p c", t=PACK)
+        res_t = []
+        for t, tenant in enumerate(("xq_plane", "x_plane1", "x_codes0", "x_codes1")):
+            rows = room("res%d" % t, [P, T], F32, tag=tenant)
+            nc.sync.dma_start(out=rows[:], in_=res_rows[t])
+            res_t.append(rows)
+        wm_codes = room("wm_codes", [P, M], I32, tag="wa_codes")
+        nc.sync.dma_start(out=wm_codes[:], in_=wm_words[0].rearrange("p c r -> p (c r)").bitcast(I32))
+        wm_plane = room("wm_plane", [P, 1, M], U8, tag="wa_plane")
+        nc.gpsimd.memset(wm_plane[:].bitcast(I32), 0)
+        load_plane(nc, wm_plane, wm_scales)
+        bias = room("bias", [P, M // P], F32, tag="x_plane0")
+        with nc.allow_non_contiguous_dma(reason="one bias value a partition"):
+            nc.sync.dma_start(out=bias[:], in_=b.rearrange("(c p) o -> p (c o)", p=P))
+
+        up = [room("up%d" % t, [P, T], F32) for t in range(PACK)]
         for t in range(PACK):
             page = pages[t % PAGES]
             if t == 0:
                 for h in range(2):
-                    nc.vector.tensor_copy(page[:].indirect(list1[:, h * 16 : (h + 1) * 16]), p_first[h][:])
+                    nc.vector.tensor_copy(page[:].indirect(entries(list1, h * HALF, HALF)), p_first[h][:])
             else:
                 nc.vector.tensor_copy(page[:].indirect(list1[:]), p_rest[t - 1][:])
-            if ADD_ON == "pe":
-                for a in range(2):
-                    acc = bank(4 + a)
-                    for n, source in enumerate((res_t[t], page)):
-                        for c in range(4):
-                            nc.tensor.matmul(
-                                acc[:, c * P : (c + 1) * P],
-                                source[:, a * BANK + c * P : a * BANK + (c + 1) * P],
-                                ident[:],
-                                start=(n == 0 and c == 0),
-                                stop=(n == 1 and c == 3),
-                                is_transpose=True,
-                            )
-                    nc.scalar.copy(turned[a][:], acc[:])
-                for a in range(2):
-                    back = bank(6 + a)
-                    for c in range(4):
-                        nc.tensor.transpose(back[:, c * P : (c + 1) * P], turned[a][:, c * P : (c + 1) * P], ident[:])
-                    nc.scalar.copy(up[t][:, a * BANK : (a + 1) * BANK], back[:])
-            else:
-                nc.gpsimd.tensor_tensor(up[t][:], res_t[t][:], page[:], ADD)
+            nc.gpsimd.tensor_tensor(up[t][:], res_t[t][:], page[:], ADD)
 
-        picked = keep.tile([P, 2, PACK, HALF], BF16, name="picked", align_bytes=64)
-        for t in range(2):
-            nc.vector.tensor_copy(picked[:, :, t, :], up[t][:].indirect(list2[:]))
-        for h in range(2):
-            for t in range(2, PACK):
-                nc.vector.tensor_copy(picked[:, h, t, :], up[t][:].indirect(list2[:, h * 16 : (h + 1) * 16]))
+        early = room("picked_early", [P, PIECES - 1, SLOTS, PIECE], BF16)
+        last = room("picked_last", [P, SLOTS, PIECE], BF16, tag="x_codes1")
+        picked = [early[:, k] for k in range(PIECES - 1)] + [last[:]]
+        woven = [picked[k + 2][:, 2:SLOTS, :] for k in range(2)]
+        woven = woven + [room("woven%d" % k, [P, PACK, PIECE], BF16)[:] for k in range(2, PIECES)]
+        out_rows = out.rearrange("(c p) i -> p c i", p=P)
 
-        woven = [keep.tile([P, HALF, PACK], BF16, name="woven%d" % h, align_bytes=64) for h in range(2)]
-        for h in range(2):
-            dst = woven[h][:].rearrange("p (c i) t -> p c t i", i=4)
-            src = picked[:, h].rearrange("p t (c i) -> p c t i", i=4)
-            if h == 0:
+        def pick(t, k):
+            nc.vector.tensor_copy(picked[k][:, t, :], up[t][:].indirect(entries(list2, k * PIECE, PIECE)))
+
+        def weave(k):
+            dst = woven[k].rearrange("p s w -> p (s w)").rearrange("p (c i t) -> p c t i", i=4, t=PACK)
+            src = picked[k][:, 0:PACK, :].rearrange("p t (c i) -> p c t i", i=4)
+            if k < PIECES - 1:
                 nc.scalar.copy(dst, src)
             else:
                 nc.vector.tensor_copy(dst, src)
-        out_rows = out.rearrange("(c p) i -> p c i", p=P)
-        for h in range(2):
-            u_codes = keep.tile([P, HALF], U32, name="u_codes%d" % h, align_bytes=64)
-            u_plane = keep.tile([P, HALF], U8, name="u_plane%d" % h, align_bytes=64)
+
+        def second_product(k):
+            u_codes = room("u_codes%d" % k, [P, PIECE], U32)
+            u_plane = room("u_plane%d" % k, [P, PIECE], U8)
             nc.vector.quantize_mx(
-                out=u_codes[:].bitcast(FP8X4), scales=u_plane[:], in_=woven[h][:].rearrange("p c t -> p (c t)")
+                out=u_codes[:].bitcast(FP8X4), scales=u_plane[:], in_=woven[k].rearrange("p s w -> p (s w)")
             )
+            if k < PIECES - 1:
+                pair = [bank(2 * k + g) for g in range(2)]
+                sums = [pair[c // 2][:, (c % 2) * PIECE : (c % 2 + 1) * PIECE] for c in range(M // P)]
+            else:
+                sums = [bank((2 * k + c) % 8)[:, 0:PIECE] for c in range(M // P)]
+            for c in range(M // P):
+                nc.tensor.matmul_mx(
+                    out=sums[c],
+                    lhsT=wm_codes[:, c * P : (c + 1) * P].bitcast(FP8X4),
+                    lhsT_scale=wm_plane[:, 0, c * P : (c + 1) * P],
+                    rhs=u_codes[:].bitcast(FP8X4),
+                    rhs_scale=u_plane[:],
+                    start=True,
+                    stop=True,
+                )
+            return sums
+
+        def finish(k, sums):
             for g in range(2):
-                acc = bank(2 * h + g)
-                y = keep.tile([P, 2, HALF], F32, name="y%d_%d" % (h, g), align_bytes=64)
+                y = room("y%d_%d" % (k, g), [P, 2, PIECE], F32)
                 for e in range(2):
                     c = 2 * g + e
-                    nc.tensor.matmul_mx(
-                        out=acc[:, e * HALF : (e + 1) * HALF],
-                        lhsT=wm_codes[:, c * P : (c + 1) * P].bitcast(FP8X4),
-                        lhsT_scale=wm_plane[:, 0, c * P : (c + 1) * P],
-                        rhs=u_codes[:].bitcast(FP8X4),
-                        rhs_scale=u_plane[:],
-                        start=True,
-                        stop=True,
-                    )
-                for e in range(2):
-                    c = 2 * g + e
-                    if g == 0 or h == 0:
-                        nc.scalar.activation(y[:, e, :], acc[:, e * HALF : (e + 1) * HALF], RELU, bias=bias[:, c : c + 1])
+                    if k == PIECES - 1 and e == 1:
+                        nc.vector.tensor_scalar(y[:, e, :], sums[c], bias[:, c : c + 1], 0.0, ADD, MAX)
                     else:
-                        nc.vector.tensor_scalar(
-                            y[:, e, :], acc[:, e * HALF : (e + 1) * HALF], bias[:, c : c + 1], 0.0, ADD, MAX
-                        )
-                nc.sync.dma_start(out=out_rows[:, 2 * g : 2 * g + 2, h * HALF : (h + 1) * HALF], in_=y[:])
+                        nc.scalar.activation(y[:, e, :], sums[c], RELU, bias=bias[:, c : c + 1])
+                nc.sync.dma_start(out=out_rows[:, 2 * g : 2 * g + 2, k * PIECE : (k + 1) * PIECE], in_=y[:])
+
+        for t in range(2):
+            nc.vector.tensor_copy(early[:, :, t, :], up[t][:].indirect(entries(list2, 0, 3 * PIECE)))
+        nc.vector.tensor_copy(early[:, 0:2, 2, :], up[2][:].indirect(entries(list2, 0, 2 * PIECE)))
+        pick(3, 0)
+        pick(3, 1)
+        weave(0)
+        pick(0, 3)
+        pick(1, 3)
+        weave(1)
+        sums = []
+        for k in range(2):
+            sums.append(second_product(k))
+            pick(2, k + 2)
+            pick(3, k + 2)
+            weave(k + 2)
+        for k in range(2, PIECES):
+            sums.append(second_product(k))
+        for k in range(PIECES):
+            finish(k, sums[k])

@@ -26,7 +26,7 @@ HALF = J // 2
 PAGES = 3
 PIECE = 128
 PIECES = I // PIECE
-SLOTS = 6
+SLOTS = 7
 
 
 def load_plane(nc, plane, scales):
@@ -58,49 +58,60 @@ def tile_list_second_reads_updated_page_kernel(
 
         list1 = lists.tile([P, J // 16], U16, name="list1")
         list2 = lists.tile([P, I // 16], U16, name="list2")
-        xq_plane = room("xq_plane", [P, PASSES, T], U8)
+        xq_planes = room("xq_planes", [P, T], U8)
+        x_plane_moved = room("x_plane_moved", [P, J], U8)
         wa_plane_raw = room("wa_plane_raw", [P, PASSES, N], U8)
         wa_raw = [room("wa_raw%d" % z, [P, 2 * N], U8) for z in range(PASSES)]
-        xq_tab = room("xq_tab", [P, PASSES, T], I32)
+        xq_tab = [room("xq_tab%d" % z, [P, T], I32) for z in range(PASSES)]
         pages = [room("page0", [P, T], F32)]
 
-        nc.vector.memset(xq_plane[:, 0, :].bitcast(I32), 0)
-        nc.gpsimd.memset(xq_plane[:, 1, :].bitcast(I32), 0)
+        nc.vector.memset(xq_planes[:].bitcast(I32), 0)
         nc.vector.memset(wa_plane_raw[:].bitcast(I32), 0)
+        nc.vector.memset(x_plane_moved[:].bitcast(I32), 0)
         nc.vector.memset(pages[0][:], 0.0)
 
         nc.sync.dma_start(out=list1[:], in_=offs)
         for z in range(PASSES):
             nc.sync.dma_start(out=wa_raw[z][:].bitcast(I32), in_=wa_words[z].bitcast(I32))
         nc.sync.dma_start(out=list2[:], in_=offs2)
-        load_plane(nc, xq_plane, xq_scales)
+        for q in range(4):
+            nc.sync.dma_start(
+                out=xq_planes[32 * q : 32 * q + 8, :].bitcast(I32), in_=xq_scales[:, 4 * q : 4 * q + 4, :].bitcast(I32)
+            )
+        nc.sync.dma_start(out=xq_tab[0][:], in_=xq_words[0].rearrange("p c r -> p (c r)").bitcast(I32))
         load_plane(nc, wa_plane_raw, wa_scales)
-        nc.sync.dma_start(out=xq_tab[:], in_=xq_words.rearrange("z p c r -> p z (c r)").bitcast(I32))
+        nc.sync.dma_start(out=xq_tab[1][:], in_=xq_words[1].rearrange("p c r -> p (c r)").bitcast(I32))
 
         wa_codes = room("wa_codes", [P, PASSES, 2 * N], U8)
-        wa_plane = room("wa_plane", [P, PASSES, N], U8)
+        wa_plane_first = room("wa_plane_first", [P, PASSES, 1, P], U8)
         x_codes = [room("x_codes%d" % z, [P, J], U32) for z in range(PASSES)]
-        x_plane = [room("x_plane%d" % z, [P, J], U8) for z in range(PASSES)]
+        x_planes = room("x_planes", [P, J], U8)
+        x_plane = [x_planes, x_plane_moved]
 
         for z in range(PASSES):
             nc.vector.tensor_copy(
                 wa_codes[:, z, :].bitcast(U16).rearrange("p (t m) -> p t m", t=PACK),
                 wa_raw[z][:].bitcast(U16).rearrange("p (m t) -> p t m", t=PACK),
             )
-        for z in range(PASSES):
-            nc.vector.tensor_copy(x_plane[z][:], xq_plane[:, z, :].indirect(list1[:]))
-        nc.vector.tensor_copy(
-            wa_plane[:].rearrange("p z (t m) -> p z t m", t=PACK),
-            wa_plane_raw[:].rearrange("p z (m t) -> p z t m", t=PACK),
-        )
+        nc.vector.tensor_copy(x_planes[:], xq_planes[:].indirect(list1[:]))
+        for q in range(4):
+            nc.scalar.dma_start(
+                out=x_plane_moved[32 * q : 32 * q + 4, :].bitcast(I32),
+                in_=x_planes[32 * q + 4 : 32 * q + 8, :].bitcast(I32),
+            )
+        wa_plane_dealt = wa_plane_raw[:].rearrange("p z (m t) -> p z t m", t=PACK)
+        nc.vector.tensor_copy(wa_plane_first[:], wa_plane_dealt[:, :, 0:1, :])
+        nc.vector.tensor_copy(x_codes[0][:], xq_tab[0][:].bitcast(U32).indirect(list1[:]))
         for h in range(2):
-            for z in range(PASSES):
-                nc.vector.tensor_copy(
-                    x_codes[z][:, h * HALF : (h + 1) * HALF],
-                    xq_tab[:, z, :].bitcast(U32).indirect(entries(list1, h * HALF, HALF)),
-                )
+            nc.vector.tensor_copy(
+                x_codes[1][:, h * HALF : (h + 1) * HALF],
+                xq_tab[1][:].bitcast(U32).indirect(entries(list1, h * HALF, HALF)),
+            )
+        wa_plane_rest = room("wa_plane_rest", [P, PASSES, PACK - 1, P], U8, tag="xq_tab1")
+        nc.vector.tensor_copy(wa_plane_rest[:], wa_plane_dealt[:, :, 1:PACK, :])
+        wa_plane = [wa_plane_first[:, :, 0, :]] + [wa_plane_rest[:, :, t, :] for t in range(PACK - 1)]
 
-        for tenant in ("wa_plane_raw", "xq_tab"):
+        for tenant in ("xq_planes", "wa_plane_raw"):
             page = room("page%d" % len(pages), [P, T], F32, tag=tenant)
             nc.gpsimd.memset(page[:], 0.0)
             pages.append(page)
@@ -111,7 +122,7 @@ def tile_list_second_reads_updated_page_kernel(
                 nc.tensor.matmul_mx(
                     out=acc[:, lo : lo + width],
                     lhsT=wa_codes[:, z, 2 * P * t : 2 * P * (t + 1)].bitcast(FP4X4),
-                    lhsT_scale=wa_plane[:, z, P * t : P * (t + 1)],
+                    lhsT_scale=wa_plane[t][:, z, :],
                     rhs=x_codes[z][:, first + lo : first + lo + width].bitcast(FP8X4),
                     rhs_scale=x_plane[z][:, first + lo : first + lo + width],
                     start=((z, lo) == steps[0]),
@@ -135,16 +146,16 @@ def tile_list_second_reads_updated_page_kernel(
 
         res_rows = res.rearrange("(p t) c -> t p c", t=PACK)
         res_t = []
-        for t, tenant in enumerate(("xq_plane", "x_plane1", "x_codes0", "x_codes1")):
+        for t, tenant in enumerate(("xq_tab0", "x_plane_moved", "x_codes0", "x_codes1")):
             rows = room("res%d" % t, [P, T], F32, tag=tenant)
             nc.sync.dma_start(out=rows[:], in_=res_rows[t])
             res_t.append(rows)
         wm_codes = room("wm_codes", [P, M], I32, tag="wa_codes")
         nc.sync.dma_start(out=wm_codes[:], in_=wm_words[0].rearrange("p c r -> p (c r)").bitcast(I32))
-        wm_plane = room("wm_plane", [P, 1, M], U8, tag="wa_plane")
+        wm_plane = room("wm_plane", [P, 1, M], U8, tag="wa_plane_first")
         nc.gpsimd.memset(wm_plane[:].bitcast(I32), 0)
         load_plane(nc, wm_plane, wm_scales)
-        bias = room("bias", [P, M // P], F32, tag="x_plane0")
+        bias = room("bias", [P, M // P], F32, tag="x_planes")
         with nc.allow_non_contiguous_dma(reason="one bias value a partition"):
             nc.sync.dma_start(out=bias[:], in_=b.rearrange("(c p) o -> p (c o)", p=P))
 
@@ -161,14 +172,15 @@ def tile_list_second_reads_updated_page_kernel(
         early = room("picked_early", [P, PIECES - 1, SLOTS, PIECE], BF16)
         last = room("picked_last", [P, SLOTS, PIECE], BF16, tag="x_codes1")
         picked = [early[:, k] for k in range(PIECES - 1)] + [last[:]]
-        woven = [picked[k + 2][:, 2:SLOTS, :] for k in range(2)]
-        woven = woven + [room("woven%d" % k, [P, PACK, PIECE], BF16)[:] for k in range(2, PIECES)]
+        woven = [picked[2][:, 3:7, :], picked[3][:, 2:6, :]]
         out_rows = out.rearrange("(c p) i -> p c i", p=P)
 
         def pick(t, k):
             nc.vector.tensor_copy(picked[k][:, t, :], up[t][:].indirect(entries(list2, k * PIECE, PIECE)))
 
         def weave(k):
+            if k >= 2:
+                woven.append(room("woven%d" % k, [P, PACK, PIECE], BF16, tag="woven")[:])
             dst = woven[k].rearrange("p s w -> p (s w)").rearrange("p (c i t) -> p c t i", i=4, t=PACK)
             src = picked[k][:, 0:PACK, :].rearrange("p t (c i) -> p c t i", i=4)
             if k < PIECES - 1:
@@ -210,22 +222,22 @@ def tile_list_second_reads_updated_page_kernel(
                         nc.scalar.activation(y[:, e, :], sums[c], RELU, bias=bias[:, c : c + 1])
                 nc.sync.dma_start(out=out_rows[:, 2 * g : 2 * g + 2, k * PIECE : (k + 1) * PIECE], in_=y[:])
 
-        for t in range(2):
+        for t in range(3):
             nc.vector.tensor_copy(early[:, :, t, :], up[t][:].indirect(entries(list2, 0, 3 * PIECE)))
-        nc.vector.tensor_copy(early[:, 0:2, 2, :], up[2][:].indirect(entries(list2, 0, 2 * PIECE)))
         pick(3, 0)
         pick(3, 1)
         weave(0)
         pick(0, 3)
         pick(1, 3)
         weave(1)
-        sums = []
-        for k in range(2):
-            sums.append(second_product(k))
-            pick(2, k + 2)
-            pick(3, k + 2)
-            weave(k + 2)
-        for k in range(2, PIECES):
-            sums.append(second_product(k))
+        sums = [second_product(0)]
+        pick(3, 2)
+        weave(2)
+        sums.append(second_product(1))
+        pick(2, 3)
+        pick(3, 3)
+        sums.append(second_product(2))
+        weave(3)
+        sums.append(second_product(3))
         for k in range(PIECES):
             finish(k, sums[k])

from contextlib import ExitStack

import concourse.mybir as mybir

K, T, J, I, N, M = 1024, 1024, 512, 512, 512, 512
FLOPS = 2 * K * N * J + 2 * N * M * I

F32 = mybir.dt.float32
BF16 = mybir.dt.bfloat16
I32 = mybir.dt.int32
U32 = mybir.dt.uint32
U16 = mybir.dt.uint16
U8 = mybir.dt.uint8
FP8X4 = mybir.dt.float8_e4m3fn_x4
FP4X4 = mybir.dt.float4_e2m1fn_x4
ADD = mybir.AluOpType.add
MAX = mybir.AluOpType.max
COPY = mybir.ActivationFunctionType.Copy
RELU = mybir.ActivationFunctionType.Relu

P = 128
PACK = 4
PASSES = K // (P * PACK)
BANK = 512
HALF = J // 2
PAGES = 3
PIECE = 128
PIECES = I // PIECE
SLOTS = 7


def load_plane(nc, plane, scales):
    for q in range(4):
        nc.sync.dma_start(
            out=plane[32 * q : 32 * q + 4].bitcast(I32),
            in_=scales[:, 4 * q : 4 * q + 4, :].rearrange("z r c -> r z c").bitcast(I32),
        )


def entries(offsets, first, count):
    return offsets[:, first // 16 : (first + count) // 16]


def tile_list_second_reads_updated_page_kernel(
    tc, xq_words, xq_scales, wa_words, wa_scales, res, wm_words, wm_scales, b, offs, offs2, out
):
    nc = tc.nc
    with ExitStack() as ctx:
        lists = ctx.enter_context(tc.tile_pool(name="lists", bufs=1))
        keep = ctx.enter_context(tc.tile_pool(name="keep", bufs=1))
        psum = ctx.enter_context(tc.psum_pool(name="psum", bufs=1))

        def bank(index):
            return psum.tile([P, BANK], F32, name="bank%d" % index)

        def room(name, shape, dtype, tag=None):
            return keep.tile(shape, dtype, name=name, tag=tag or name, align_bytes=64)

        list1 = lists.tile([P, J // 16], U16, name="list1")
        list2 = lists.tile([P, I // 16], U16, name="list2")
        xq_planes = room("xq_planes", [P, T], U8)
        x_plane_moved = room("x_plane_moved", [P, J], U8)
        wa_plane_raw = room("wa_plane_raw", [P, PASSES, N], U8)
        wa_raw = [room("wa_raw%d" % z, [P, 2 * N], U8) for z in range(PASSES)]
        xq_tab = [room("xq_tab%d" % z, [P, T], I32) for z in range(PASSES)]
        pages = [room("page0", [P, T], F32)]

        nc.vector.memset(xq_planes[:].bitcast(I32), 0)
        nc.vector.memset(wa_plane_raw[:].bitcast(I32), 0)
        nc.vector.memset(x_plane_moved[:].bitcast(I32), 0)
        nc.vector.memset(pages[0][:], 0.0)

        nc.sync.dma_start(out=list1[:], in_=offs)
        for z in range(PASSES):
            nc.sync.dma_start(out=wa_raw[z][:].bitcast(I32), in_=wa_words[z].bitcast(I32))
        nc.sync.dma_start(out=list2[:], in_=offs2)
        for q in range(4):
            nc.sync.dma_start(
                out=xq_planes[32 * q : 32 * q + 8, :].bitcast(I32), in_=xq_scales[:, 4 * q : 4 * q + 4, :].bitcast(I32)
            )
        nc.sync.dma_start(out=xq_tab[0][:], in_=xq_words[0].rearrange("p c r -> p (c r)").bitcast(I32))
        load_plane(nc, wa_plane_raw, wa_scales)
        nc.sync.dma_start(out=xq_tab[1][:], in_=xq_words[1].rearrange("p c r -> p (c r)").bitcast(I32))

        wa_codes = room("wa_codes", [P, PASSES, 2 * N], U8)
        wa_plane_first = room("wa_plane_first", [P, PASSES, 1, P], U8)
        x_codes = [room("x_codes%d" % z, [P, J], U32) for z in range(PASSES)]
        x_planes = room("x_planes", [P, J], U8)
        x_plane = [x_planes, x_plane_moved]

        for z in range(PASSES):
            nc.vector.tensor_copy(
                wa_codes[:, z, :].bitcast(U16).rearrange("p (t m) -> p t m", t=PACK),
                wa_raw[z][:].bitcast(U16).rearrange("p (m t) -> p t m", t=PACK),
            )
        nc.vector.tensor_copy(x_planes[:], xq_planes[:].indirect(list1[:]))
        for q in range(4):
            nc.scalar.dma_start(
                out=x_plane_moved[32 * q : 32 * q + 4, :].bitcast(I32),
                in_=x_planes[32 * q + 4 : 32 * q + 8, :].bitcast(I32),
            )
        wa_plane_dealt = wa_plane_raw[:].rearrange("p z (m t) -> p z t m", t=PACK)
        nc.vector.tensor_copy(wa_plane_first[:], wa_plane_dealt[:, :, 0:1, :])
        nc.vector.tensor_copy(x_codes[0][:], xq_tab[0][:].bitcast(U32).indirect(list1[:]))
        for h in range(2):
            nc.vector.tensor_copy(
                x_codes[1][:, h * HALF : (h + 1) * HALF],
                xq_tab[1][:].bitcast(U32).indirect(entries(list1, h * HALF, HALF)),
            )
        wa_plane_rest = room("wa_plane_rest", [P, PASSES, PACK - 1, P], U8, tag="xq_tab1")
        nc.vector.tensor_copy(wa_plane_rest[:], wa_plane_dealt[:, :, 1:PACK, :])
        wa_plane = [wa_plane_first[:, :, 0, :]] + [wa_plane_rest[:, :, t, :] for t in range(PACK - 1)]

        for tenant in ("xq_planes", "wa_plane_raw"):
            page = room("page%d" % len(pages), [P, T], F32, tag=tenant)
            nc.gpsimd.memset(page[:], 0.0)
            pages.append(page)

        def first_product(acc, t, first, count, width):
            steps = [(z, lo) for z in range(PASSES) for lo in range(0, count, width)]
            for z, lo in steps:
                nc.tensor.matmul_mx(
                    out=acc[:, lo : lo + width],
                    lhsT=wa_codes[:, z, 2 * P * t : 2 * P * (t + 1)].bitcast(FP4X4),
                    lhsT_scale=wa_plane[t][:, z, :],
                    rhs=x_codes[z][:, first + lo : first + lo + width].bitcast(FP8X4),
                    rhs_scale=x_plane[z][:, first + lo : first + lo + width],
                    start=((z, lo) == steps[0]),
                    stop=((z, lo) == steps[-1]),
                )

        p_first = []
        for h in range(2):
            acc = bank(h)
            first_product(acc, 0, h * HALF, HALF, P)
            p_half = room("p0_%d" % h, [P, HALF], F32)
            nc.scalar.activation(p_half[:], acc[:, 0:HALF], COPY)
            p_first.append(p_half)
        p_rest = []
        for t in range(1, PACK):
            acc = bank(t + 1)
            first_product(acc, t, 0, J, J)
            p_t = room("p%d" % t, [P, J], F32)
            nc.scalar.copy(p_t[:], acc[:])
            p_rest.append(p_t)

        res_rows = res.rearrange("(p t) c -> t p c", t=PACK)
        res_t = []
        for t, tenant in enumerate(("xq_tab0", "x_plane_moved", "x_codes0", "x_codes1")):
            rows = room("res%d" % t, [P, T], F32, tag=tenant)
            nc.sync.dma_start(out=rows[:], in_=res_rows[t])
            res_t.append(rows)
        wm_codes = room("wm_codes", [P, M], I32, tag="wa_codes")
        nc.sync.dma_start(out=wm_codes[:], in_=wm_words[0].rearrange("p c r -> p (c r)").bitcast(I32))
        wm_plane = room("wm_plane", [P, 1, M], U8, tag="wa_plane_first")
        nc.gpsimd.memset(wm_plane[:].bitcast(I32), 0)
        load_plane(nc, wm_plane, wm_scales)
        bias = room("bias", [P, M // P], F32, tag="x_planes")
        with nc.allow_non_contiguous_dma(reason="one bias value a partition"):
            nc.sync.dma_start(out=bias[:], in_=b.rearrange("(c p) o -> p (c o)", p=P))

        up = [room("up%d" % t, [P, T], F32) for t in range(PACK)]
        for t in range(PACK):
            page = pages[t % PAGES]
            if t == 0:
                for h in range(2):
                    nc.vector.tensor_copy(page[:].indirect(entries(list1, h * HALF, HALF)), p_first[h][:])
            else:
                nc.vector.tensor_copy(page[:].indirect(list1[:]), p_rest[t - 1][:])
            nc.gpsimd.tensor_tensor(up[t][:], res_t[t][:], page[:], ADD)

        early = room("picked_early", [P, PIECES - 1, SLOTS, PIECE], BF16)
        last = room("picked_last", [P, SLOTS, PIECE], BF16, tag="x_codes1")
        picked = [early[:, k] for k in range(PIECES - 1)] + [last[:]]
        woven = [picked[2][:, 3:7, :], picked[3][:, 2:6, :]]
        out_rows = out.rearrange("(c p) i -> p c i", p=P)

        def pick(t, k):
            nc.vector.tensor_copy(picked[k][:, t, :], up[t][:].indirect(entries(list2, k * PIECE, PIECE)))

        def weave(k):
            if k >= 2:
                woven.append(room("woven%d" % k, [P, PACK, PIECE], BF16, tag="woven")[:])
            dst = woven[k].rearrange("p s w -> p (s w)").rearrange("p (c i t) -> p c t i", i=4, t=PACK)
            src = picked[k][:, 0:PACK, :].rearrange("p t (c i) -> p c t i", i=4)
            if k < PIECES - 1:
                nc.scalar.copy(dst, src)
            else:
                nc.vector.tensor_copy(dst, src)

        def second_product(k):
            u_codes = room("u_codes%d" % k, [P, PIECE], U32)
            u_plane = room("u_plane%d" % k, [P, PIECE], U8)
            nc.vector.quantize_mx(
                out=u_codes[:].bitcast(FP8X4), scales=u_plane[:], in_=woven[k].rearrange("p s w -> p (s w)")
            )
            if k < PIECES - 1:
                pair = [bank(2 * k + g) for g in range(2)]
                sums = [pair[c // 2][:, (c % 2) * PIECE : (c % 2 + 1) * PIECE] for c in range(M // P)]
            else:
                sums = [bank((2 * k + c) % 8)[:, 0:PIECE] for c in range(M // P)]
            for c in range(M // P):
                nc.tensor.matmul_mx(
                    out=sums[c],
                    lhsT=wm_codes[:, c * P : (c + 1) * P].bitcast(FP8X4),
                    lhsT_scale=wm_plane[:, 0, c * P : (c + 1) * P],
                    rhs=u_codes[:].bitcast(FP8X4),
                    rhs_scale=u_plane[:],
                    start=True,
                    stop=True,
                )
            return sums

        def finish(k, sums):
            for g in range(2):
                y = room("y%d_%d" % (k, g), [P, 2, PIECE], F32)
                for e in range(2):
                    c = 2 * g + e
                    if k == PIECES - 1 and e == 1:
                        nc.vector.tensor_scalar(y[:, e, :], sums[c], bias[:, c : c + 1], 0.0, ADD, MAX)
                    else:
                        nc.scalar.activation(y[:, e, :], sums[c], RELU, bias=bias[:, c : c + 1])
                nc.sync.dma_start(out=out_rows[:, 2 * g : 2 * g + 2, k * PIECE : (k + 1) * PIECE], in_=y[:])

        for t in range(3):
            nc.vector.tensor_copy(early[:, :, t, :], up[t][:].indirect(entries(list2, 0, 3 * PIECE)))
        pick(3, 0)
        pick(3, 1)
        weave(0)
        pick(0, 3)
        pick(1, 3)
        weave(1)
        sums = [second_product(0)]
        pick(3, 2)
        weave(2)
        sums.append(second_product(1))
        pick(2, 3)
        pick(3, 3)
        sums.append(second_product(2))
        weave(3)
        sums.append(second_product(3))
        for k in range(PIECES):
            finish(k, sums[k])
